import numpy as np, ml_dtypes
CORES = [10,34,74,98]
N = 4
BF = ml_dtypes.bfloat16
F, L, W, S = 32, 128, 16, 32 * 128
def latest(gl):
    i = np.arange(L); return np.max(i - (i * np.asarray(gl).astype(np.int64)[..., None] >> 5), axis=-1)
def shortest(g1, g2):
    return latest(g1) + 1, np.maximum(latest(g2) - (L - 1), 0)
def joined(w, l1, g1, l2, g2):
    return np.concatenate([w, l1, g1, l2, g2], axis=2).astype(np.int32)
def glides(rng):
    return rng.integers(-64, 97, (N, 8, F))
def lags(rng, lo):
    hi = np.maximum(lo, np.minimum(S - 1, L * np.arange(F) + L - 1)); hi = np.where(rng.random(lo.shape) < 0.125, S - 1, hi)
    return rng.integers(lo, hi + 1)
def setup_inputs(rng):
    v = rng.integers(-127, 128, (N, 128, W * L), dtype=np.int8) >> rng.integers(0, 6, (N, 128, 1), dtype=np.int8)
    g1, g2 = glides(rng), glides(rng); m1, m2 = shortest(g1, g2)
    return {"book": v.astype(np.float32).astype(BF), "par": joined(rng.integers(0, W, (N, 8, F)), lags(rng, m1), g1, lags(rng, m2), g2)}
def setup_inputs_near(rng):
    d = setup_inputs(rng); g1, g2 = glides(rng), glides(rng); m1, m2 = shortest(g1, g2)
    l1 = np.minimum(m1 + rng.integers(0, 4, m1.shape) * (rng.random(m1.shape) < 0.5), S - 1); l2 = np.minimum(m2 + rng.integers(0, 4, m2.shape) * (rng.random(m2.shape) < 0.5), S - 1)
    d["par"] = joined(rng.integers(0, W, (N, 8, F)), l1, g1, l2, g2); return d
def setup_inputs_far(rng):
    d = setup_inputs(rng); g = [np.where(rng.random((N, 8, F)) < 0.5, 0, glides(rng)) for k in range(2)]; m = shortest(g[0], g[1]); l = []
    for k in range(2):
        a = L * np.arange(F) + rng.integers(0, L, (N, 8, F)); a = np.where(rng.random(a.shape) < 0.25, S - 1 - rng.integers(0, 2, a.shape), a)
        l.append(np.minimum(np.maximum(a, m[k]), S - 1))
    d["par"] = joined(rng.integers(0, W, (N, 8, F)), l[0], g[0], l[1], g[1]); return d
def setup_inputs_ends(rng):
    d = setup_inputs(rng); e = np.array([-64, -63, -33, -32, -31, -1, 0, 1, 31, 32, 33, 63, 64, 95, 96]); g = [rng.choice(e, (N, 8, F)) for k in range(2)]; m = shortest(g[0], g[1]); l = []
    for k in range(2):
        u = rng.random((N, 8, F)); l.append(np.where(u < 0.25, m[k], np.where(u < 0.375, S - 1, lags(rng, m[k]))))
    d["par"] = joined(rng.choice(np.array([0, W - 1, W >> 1]), (N, 8, F)), l[0], g[0], l[1], g[1]); return d
def setup_inputs_loud(rng):
    d = setup_inputs(rng); v = np.array([-127, -126, 126, 127, -1, 0, 1, 127, -127], np.float32)
    d["book"] = v[rng.integers(0, 9, (N, 128, W * L), dtype=np.int8)].astype(BF); return d
def setup_inputs_spread(rng):
    d = setup_inputs(rng); v = rng.integers(-127, 128, (N, 128, W * L), dtype=np.int8) >> rng.integers(0, 8, (N, 1, W * L), dtype=np.int8)
    d["book"] = (v * (rng.random((N, 1, W * L)) > 0.0625)).astype(np.float32).astype(BF)
    w = d["par"][:, :, :F]; d["par"][:, :, :F] = np.where(rng.random(w.shape) < 0.5, rng.integers(0, W, (N, 8, 1)), w); return d
def check_inputs(d):
    b = d["book"].astype(np.float32); p = d["par"].astype(np.int64); bad = []
    w, l1, g1, l2, g2 = [p[:, :, F * k:F * k + F] for k in range(5)]
    if not ((b == np.floor(b)) & (np.abs(b) <= 127)).all(): bad.append("book")
    if not ((w >= 0) & (w < W)).all(): bad.append("words")
    if not ((l1 >= 0) & (l1 < S) & (l2 >= 0) & (l2 < S)).all(): bad.append("lags")
    if not ((g1 >= -64) & (g1 <= 96) & (g2 >= -64) & (g2 <= 96)).all(): bad.append("glides")
    if not (latest(g1) - l1 < 0).all(): bad.append("own_places")
    if not (latest(g2) - l2 < L).all(): bad.append("lower_places")
    return bad
def reference(book, par):
    w, l1, g1, l2, g2 = [par[:, :, F * k:F * k + F].astype(np.int64) for k in range(5)]
    x = np.zeros((N + 1, 8, 16, S + 1), np.float32); i = np.arange(L)
    for r in range(N):
        b = book[r].astype(np.float32).reshape(8, 16, W, L)
        for k in range(F):
            own = np.maximum(L * k + i - l1[r, :, k, None] - (i * g1[r, :, k, None] >> 5), -1) + 1
            low = np.maximum(L * k + i - l2[r, :, k, None] - (i * g2[r, :, k, None] >> 5), -1) + 1
            for g in range(8):
                v = b[g, :, w[r, g, k]] + x[r + 1, g][:, own[g]] - x[r, g][:, low[g]]
                x[r + 1, g, :, L * k + 1:L * k + L + 1] = np.minimum(np.maximum(v, np.float32(-127)), np.float32(127))
    return {"y": np.ascontiguousarray(x[1:, :, :, 1:]).reshape(N, 128, S)}

@@ -1,0 +1,252 @@
+from concourse.mybir import AluOpType, ActivationFunctionType
+
+F, L, W, S = 32, 128, 16, 4096
+PAD = 16
+K = L // 16
+BATCHES = [1, 3, 4, 4, 4, 4, 4, 4, 4]
+ON_VECTOR = tuple(sum(BATCHES[:j]) for j in range(len(BATCHES)))
+WORDS0 = [1, 2, 3, 5, 8, 12, 18, 26, 32]
+WORDS_SCALAR = 18
+MID_STORES = {0: {}, 1: {}, 2: {5: 6}}
+LAST_STORES = [4, 8, 12, 16, 20, 24, 28]
+SLOTS = max(BATCHES)
+
+SCRATCH = {
+    "bk": ("sbuf", [128, W * L], "bfloat16"),
+    "xw": ("sbuf", [128, PAD + S], "bfloat16"),
+    "lw": ("sbuf", [128, PAD + S], "bfloat16"),
+    "bw": ("sbuf", [128, S], "bfloat16"),
+    "lg": ("sbuf", [128, S], "bfloat16"),
+    "pre": ("sbuf", [128, S], "bfloat16"),
+    "tmp": ("sbuf", [128, L], "bfloat16"),
+    "tail": ("sbuf", [128, 4 * L], "float32"),
+    "pi": ("sbuf", [128, 5 * F], "int32"),
+    "pf": ("sbuf", [128, 5 * F], "float32"),
+    "cst": ("sbuf", [128, 5 * F], "float32"),
+    "w64": ("sbuf", [128, 128], "float32"),
+    "eio": ("sbuf", [128, 128], "float32"),
+    "em": ("sbuf", [128, 128], "float32"),
+    "iio": ("sbuf", [128, 128], "float32"),
+    "ident": ("sbuf", [128, 128], "bfloat16"),
+    "pa": ("sbuf", [128, K], "int32"),
+    "pq": ("sbuf", [128, K], "int32"),
+    "pb": ("sbuf", [128, K], "float32"),
+    "i8": ("sbuf", [128, K], "float32"),
+    "n32": ("sbuf", [128, K], "float32"),
+    "t1": ("sbuf", [128, 2 * F * K], "float32"),
+    "t2": ("sbuf", [128, 2 * F * K], "float32"),
+    "offb": ("sbuf", [128, F * K], "uint16"),
+    "offp": ("sbuf", [128, 2 * F * K], "uint16"),
+    "pp": ("psum", [128, 512], "float32"),
+}
+for _k in range(SLOTS):
+    SCRATCH["ps%d" % _k] = ("psum", [128, 512], "float32")
+
+SEMAPHORES = (["par", "gpar", "book", "iota", "vi", "conv", "mm", "offb", "offp", "bwv", "low", "own", "done", "sent",
+               "gst", "hst", "f32"]
+              + ["arr%d" % j for j in range(len(BATCHES))]
+              + ["bw%d" % j for j in range(len(WORDS0))]
+              + [n + str(k) for n in ("lg", "pe", "cp") for k in range(SLOTS)])
+
+
+def rank_program(g, core, T, topo):
+    r = T.rank_of(core)
+    if r is None:
+        return
+    last = r == len(T.cores) - 1
+    V, A, P, Y, sem = g.vector, g.scalar, g.tensor, g.sync, T.sem
+    op, Copy = AluOpType, ActivationFunctionType.Copy
+    n = {}
+
+    def inc(ins, name):
+        n[name] = n.get(name, 0) + 1
+        ins.then_inc(sem[name], 1)
+
+    def fr(t, f0, f1, pad=0):
+        return t[:, pad + L * f0:pad + L * f1]
+
+    def words(f0, f1):
+        return T.bk[:, :].indirect(T.offb[:, K * f0:K * f1])
+
+    def own(f):
+        return T.xw[:, 0:PAD + L * f].indirect(T.offp[:, K * f:K * f + K])
+
+    def lower(f):
+        return T.lw[:, 0:PAD + L * (f + 1)].indirect(T.offp[:, K * (F + f):K * (F + f) + K])
+
+    lists = 1 if r == 0 else 2
+    ca, cd, nc = F, F + lists * F, F + 2 * lists * F
+    starts = [sum(BATCHES[:j]) for j in range(len(BATCHES) + 1)]
+    batch_of = [j for j, b in enumerate(BATCHES) for _ in range(b)]
+
+    par_sem = "gpar" if r >= 2 else "par"
+    (g if r >= 2 else Y).dma_start(T.pi[0:8, :], T.par[:, :]).then_inc(sem[par_sem], 16)
+    Y.dma_start(T.bk[:, :], T.book[:, :]).then_inc(sem.book, 16)
+
+    fl = {"allow_small_or_imprecise_dtypes": True}
+    inc(g.iota(T.eio[0:8, :], [[1, 8], [0, 16]], 0, -1, **fl), "iota")
+    inc(g.iota(T.cst[0:1, ca:cd], [[0, lists], [-64 * L, F]], -(64 * PAD + 31), 0, **fl), "iota")
+    inc(g.iota(T.pa[:, :], [[0, K]], 0, 1), "iota")
+    inc(g.iota(T.pb[:, :], [[16, K]], 0, 0, **fl), "iota")
+    if r:
+        inc(g.iota(T.iio[:, :], [[-1, 128]], 0, 1, **fl), "iota")
+    inc(V.memset(T.cst[0:1, 0:ca], 0.0), "vi")
+    inc(V.memset(T.cst[0:1, cd:nc], -32.0 * 64), "vi")
+    inc(V.memset(T.w64[0:1, :], 1.0 / 64), "vi")
+    inc(V.memset(T.xw[:, 0:PAD], 0.0), "vi")
+    if r:
+        inc(V.memset(T.lw[:, 0:PAD], 0.0), "vi")
+    V.wait_ge(sem.iota, n["iota"])
+    inc(V.tensor_scalar(T.pq[:, :], T.pa[:, :], 15, None, op.bitwise_and), "vi")
+    inc(V.tensor_scalar(T.em[0:8, :], T.eio[0:8, :], 0.0, None, op.is_equal), "vi")
+    if r:
+        inc(V.tensor_scalar(T.ident[:, :], T.iio[:, :], 0.0, None, op.is_equal), "vi")
+    V.wait_ge(sem.vi, n["vi"])
+    made = n["vi"]
+    inc(V.tensor_tensor(T.i8[:, :], T.pq[:, :], T.pb[:, :], op.add), "vi")
+    V.wait_ge(sem.vi, n["vi"])
+    inc(V.tensor_scalar(T.n32[:, :], T.i8[:, :], -1.0 / 32, None, op.mult), "vi")
+
+    V.wait_ge(sem[par_sem], 16)
+    if r == 0:
+        moves = [(0, 0, 3 * F)]
+    else:
+        moves = [(0, 0, 2 * F), (2 * F, 3 * F, F), (3 * F, 2 * F, F), (4 * F, 4 * F, F)]
+    for to, frm, w in moves:
+        inc(V.tensor_copy(T.pf[0:8, to:to + w], T.pi[0:8, frm:frm + w]), "conv")
+    P.wait_ge(sem.vi, made)
+    P.matmul(T.pp[:, 0:nc], T.w64[0:1, :], T.cst[0:1, 0:nc], True, False)
+    P.wait_ge(sem.conv, n["conv"])
+    inc(P.matmul(T.pp[:, 0:nc], T.em[0:8, :], T.pf[0:8, 0:nc], False, True), "mm")
+
+    V.wait_ge(sem.vi, n["vi"])
+    V.wait_ge(sem.mm, 1)
+    for m in range(K):
+        inc(V.tensor_scalar(T.offb[:, m::K], T.pp[:, 0:F], float(L), T.i8[:, m:m + 1], op.mult, op.add), "offb")
+
+    def frame_offsets(f):
+        return V.tensor_scalar(T.offp[:, K * f:K * f + K], T.n32[:, :], T.pp[:, cd + f:cd + f + 1],
+                               T.pp[:, ca + f:ca + f + 1], op.mult, op.subtract)
+
+    def clamp(out, in_):
+        return V.tensor_scalar(out, in_, -127.0, 127.0, op.max, op.min)
+
+    done_at = {}
+    A.wait_ge(sem.offb, K)
+    A.wait_ge(sem.book, 16)
+    if r == 0:
+        ahead = 4
+        for f in range(1, ahead + 1):
+            inc(frame_offsets(f), "done")
+        for j in range(len(WORDS0) - 1):
+            inc(A.activation(fr(T.bw, WORDS0[j], WORDS0[j + 1]), words(WORDS0[j], WORDS0[j + 1]), Copy), "bw%d" % j)
+        V.wait_ge(sem.offb, K)
+        V.wait_ge(sem.book, 16)
+        inc(V.tensor_copy(fr(T.xw, 0, 1, PAD), words(0, 1)), "done")
+        done_at[0] = n["done"]
+        for f in range(1, F):
+            if f in WORDS0:
+                V.wait_ge(sem["bw%d" % WORDS0.index(f)], 1)
+            V.wait_ge(sem.done, n["done"])
+            inc(V.tensor_tensor(T.tmp[:, :], own(f), fr(T.bw, f, f + 1), op.add), "own")
+            if ahead <= f < F - 1:
+                inc(frame_offsets(f + 1), "done")
+            V.wait_ge(sem.own, n["own"])
+            inc(clamp(fr(T.xw, f, f + 1, PAD), T.tmp[:, :]), "done")
+            done_at[f] = n["done"]
+    else:
+        inc(A.activation(fr(T.bw, 0, WORDS_SCALAR), words(0, WORDS_SCALAR), Copy), "bw0")
+        for m in range(K):
+            inc(V.tensor_scalar(T.t1[:, m::K], T.pp[:, cd:nc], T.n32[:, m:m + 1], None, op.mult), "offp")
+        V.wait_ge(sem.offp, n["offp"])
+        for m in range(K):
+            inc(V.tensor_tensor(T.t2[:, m::K], T.t1[:, m::K], T.pp[:, ca:cd], op.subtract), "offp")
+        V.wait_ge(sem.offp, n["offp"])
+        inc(V.tensor_copy(T.offp[:, :], T.t2[:, :]), "offp")
+        V.wait_ge(sem.offb, K)
+        V.wait_ge(sem.book, 16)
+        inc(V.tensor_copy(fr(T.bw, WORDS_SCALAR, F), words(WORDS_SCALAR, F)), "bwv")
+        V.wait_ge(sem.offp, n["offp"])
+        V.wait_ge(sem.bw0, 1)
+        V.wait_ge(sem.bwv, 1)
+        A.wait_ge(sem.offp, n["offp"])
+        P.wait_ge(sem.bw0, 1)
+        P.wait_ge(sem.bwv, 1)
+
+        engines = len(topo.engines(T.cores[r - 1], core))
+        pre_at = {}
+        for j in range(len(BATCHES)):
+            A.wait_ge(sem["arr%d" % j], engines)
+            fs = [f for f in range(starts[j], starts[j + 1]) if f not in ON_VECTOR]
+            for k, f in enumerate(fs):
+                if n.get("cp%d" % k):
+                    P.wait_ge(sem["cp%d" % k], n["cp%d" % k])
+                P.matmul(T["ps%d" % k][:, 0:L], T.ident[:, :], fr(T.bw, f, f + 1), True, False)
+            for k in range(len(fs) + 1):
+                if k < len(fs):
+                    f = fs[k]
+                    inc(A.activation(fr(T.lg, f, f + 1), lower(f), Copy, scale=-1.0), "lg%d" % k)
+                    P.wait_ge(sem["lg%d" % k], n["lg%d" % k])
+                    inc(P.matmul(T["ps%d" % k][:, 0:L], T.ident[:, :], fr(T.lg, f, f + 1), False, True), "pe%d" % k)
+                if k > 0:
+                    f = fs[k - 1]
+                    A.wait_ge(sem["pe%d" % (k - 1)], n["pe%d" % (k - 1)])
+                    inc(A.activation(fr(T.pre, f, f + 1), T["ps%d" % (k - 1)][:, 0:L], Copy), "cp%d" % (k - 1))
+                    pre_at[f] = ("cp%d" % (k - 1), n["cp%d" % (k - 1)])
+
+        seen = 0
+        for f in range(F):
+            out = fr(T.xw, f, f + 1, PAD)
+            if last and f == F - 1:
+                out = fr(T.tail, 3, 4)
+            if f in ON_VECTOR:
+                while seen <= batch_of[f]:
+                    V.wait_ge(sem["arr%d" % seen], engines)
+                    seen += 1
+                inc(V.tensor_tensor(fr(T.pre, f, f + 1), lower(f), fr(T.bw, f, f + 1), op.subtract), "low")
+                pre_at[f] = ("low", n["low"])
+            if f:
+                V.wait_ge(sem.done, n["done"])
+            V.wait_ge(sem[pre_at[f][0]], pre_at[f][1])
+            if f == 0:
+                inc(V.tensor_scalar(T.tmp[:, :], fr(T.pre, 0, 1), -1.0 if 0 in ON_VECTOR else 1.0, None, op.mult), "own")
+            else:
+                inc(V.tensor_tensor(T.tmp[:, :], own(f), fr(T.pre, f, f + 1),
+                                    op.subtract if f in ON_VECTOR else op.add), "own")
+            V.wait_ge(sem.own, n["own"])
+            inc(clamp(out, T.tmp[:, :]), "done")
+            done_at[f] = n["done"]
+
+    stored = [0, 0]
+
+    def store(f1):
+        g.dma_start(fr(T.y, stored[0], f1), fr(T.xw, stored[0], f1, PAD)).then_inc(sem.gst, 16)
+        stored[0], stored[1] = f1, stored[1] + 1
+
+    if not last:
+        dst = T.cores[r + 1]
+        rid, pid, _ = topo.addr(dst)
+        mask = topo.mask(core, dst)
+        for j in range(len(BATCHES)):
+            g.wait_ge(sem.done, done_at[starts[j + 1] - 1])
+            g.remote_dma(fr(T.lw, starts[j], starts[j + 1], PAD), fr(T.xw, starts[j], starts[j + 1], PAD),
+                         sem["arr%d" % j], sem.sent, pid, rid, mask)
+            if j in MID_STORES[r]:
+                store(MID_STORES[r][j])
+        store(F)
+        g.wait_ge(sem.sent, len(BATCHES) * len(topo.engines(core, dst)))
+    else:
+        for f1 in LAST_STORES:
+            g.wait_ge(sem.done, done_at[f1 - 1])
+            store(f1)
+        A.wait_ge(sem.done, done_at[F - 3])
+        inc(A.activation(fr(T.tail, 0, 2), fr(T.xw, F - 4, F - 2, PAD), Copy), "f32")
+        A.wait_ge(sem.f32, 1)
+        A.dma_start(fr(T.y, F - 4, F - 2), fr(T.tail, 0, 2)).then_inc(sem.hst, 16)
+        A.wait_ge(sem.done, done_at[F - 2])
+        inc(A.activation(fr(T.tail, 2, 3), fr(T.xw, F - 2, F - 1, PAD), Copy), "f32")
+        Y.wait_ge(sem.f32, 2)
+        Y.wait_ge(sem.done, done_at[F - 1])
+        Y.dma_start(fr(T.y, F - 2, F), fr(T.tail, 2, 4)).then_inc(sem.hst, 16)
+        Y.wait_ge(sem.hst, 32)
+    g.wait_ge(sem.gst, 16 * stored[1])

@@ -3,11 +3,11 @@ from concourse.mybir import AluOpType, ActivationFunctionType
 F, L, W, S = 32, 128, 16, 4096
 PAD = 16
 K = L // 16
-BATCHES = [1, 3, 4, 4, 4, 4, 4, 4, 4]
-ON_VECTOR = tuple(sum(BATCHES[:j]) for j in range(len(BATCHES)))
+BATCHES = [1] + [2] * 15 + [1]
+ON_VECTOR = (0, 1)
 WORDS0 = [1, 2, 3, 5, 8, 12, 18, 26, 32]
 WORDS_SCALAR = 18
-MID_STORES = {0: {}, 1: {}, 2: {5: 6}}
+MID_STORES = {0: {}, 1: {}, 2: {6: 4, 10: 8}}
 LAST_STORES = [4, 8, 12, 16, 20, 24, 28]
 SLOTS = max(BATCHES)
 

@@ -3,13 +3,13 @@ from concourse.mybir import AluOpType, ActivationFunctionType
 F, L, W, S = 32, 128, 16, 4096
 PAD = 16
 K = L // 16
-BATCHES = [1] + [2] * 15 + [1]
+BATCHES = [1] * 32
 ON_VECTOR = (0, 1)
 WORDS0 = [1, 2, 3, 5, 8, 12, 18, 26, 32]
-WORDS_SCALAR = 18
-MID_STORES = {0: {}, 1: {}, 2: {6: 4, 10: 8}}
+WORDS_VECTOR = 11
+MID_STORES = {0: {}, 1: {}, 2: {}}
 LAST_STORES = [4, 8, 12, 16, 20, 24, 28]
-SLOTS = max(BATCHES)
+SLOTS = 2
 
 SCRATCH = {
     "bk": ("sbuf", [128, W * L], "bfloat16"),
@@ -38,12 +38,13 @@ SCRATCH = {
     "offb": ("sbuf", [128, F * K], "uint16"),
     "offp": ("sbuf", [128, 2 * F * K], "uint16"),
     "pp": ("psum", [128, 512], "float32"),
+    "pw": ("psum", [128, 512], "float32"),
 }
 for _k in range(SLOTS):
     SCRATCH["ps%d" % _k] = ("psum", [128, 512], "float32")
 
-SEMAPHORES = (["par", "gpar", "book", "iota", "vi", "conv", "mm", "offb", "offp", "bwv", "low", "own", "done", "sent",
-               "gst", "hst", "f32"]
+SEMAPHORES = (["par", "gpar", "book", "iota", "vi", "convw", "conv", "mmw", "mm", "offb", "offp", "bwv", "low", "own",
+               "done", "sent", "gst", "hst", "f32"]
               + ["arr%d" % j for j in range(len(BATCHES))]
               + ["bw%d" % j for j in range(len(WORDS0))]
               + [n + str(k) for n in ("lg", "pe", "cp") for k in range(SLOTS)])
@@ -90,7 +91,6 @@ def rank_program(g, core, T, topo):
     inc(g.iota(T.pb[:, :], [[16, K]], 0, 0, **fl), "iota")
     if r:
         inc(g.iota(T.iio[:, :], [[-1, 128]], 0, 1, **fl), "iota")
-    inc(V.memset(T.cst[0:1, 0:ca], 0.0), "vi")
     inc(V.memset(T.cst[0:1, cd:nc], -32.0 * 64), "vi")
     inc(V.memset(T.w64[0:1, :], 1.0 / 64), "vi")
     inc(V.memset(T.xw[:, 0:PAD], 0.0), "vi")
@@ -108,21 +108,25 @@ def rank_program(g, core, T, topo):
     inc(V.tensor_scalar(T.n32[:, :], T.i8[:, :], -1.0 / 32, None, op.mult), "vi")
 
     V.wait_ge(sem[par_sem], 16)
+    inc(V.tensor_copy(T.pf[0:8, 0:F], T.pi[0:8, 0:F]), "convw")
     if r == 0:
-        moves = [(0, 0, 3 * F)]
+        moves = [(F, F, 2 * F)]
     else:
-        moves = [(0, 0, 2 * F), (2 * F, 3 * F, F), (3 * F, 2 * F, F), (4 * F, 4 * F, F)]
+        moves = [(F, F, F), (2 * F, 3 * F, F), (3 * F, 2 * F, F), (4 * F, 4 * F, F)]
     for to, frm, w in moves:
         inc(V.tensor_copy(T.pf[0:8, to:to + w], T.pi[0:8, frm:frm + w]), "conv")
     P.wait_ge(sem.vi, made)
-    P.matmul(T.pp[:, 0:nc], T.w64[0:1, :], T.cst[0:1, 0:nc], True, False)
+    P.matmul(T.pp[:, ca:nc], T.w64[0:1, :], T.cst[0:1, ca:nc], True, False)
+    P.wait_ge(sem.convw, 1)
+    inc(P.matmul(T.pw[:, 0:F], T.em[0:8, :], T.pf[0:8, 0:F], True, True), "mmw")
     P.wait_ge(sem.conv, n["conv"])
-    inc(P.matmul(T.pp[:, 0:nc], T.em[0:8, :], T.pf[0:8, 0:nc], False, True), "mm")
+    inc(P.matmul(T.pp[:, ca:nc], T.em[0:8, :], T.pf[0:8, ca:nc], False, True), "mm")
 
     V.wait_ge(sem.vi, n["vi"])
-    V.wait_ge(sem.mm, 1)
+    V.wait_ge(sem.mmw, 1)
     for m in range(K):
-        inc(V.tensor_scalar(T.offb[:, m::K], T.pp[:, 0:F], float(L), T.i8[:, m:m + 1], op.mult, op.add), "offb")
+        inc(V.tensor_scalar(T.offb[:, m::K], T.pw[:, 0:F], float(L), T.i8[:, m:m + 1], op.mult, op.add), "offb")
+    V.wait_ge(sem.mm, 1)
 
     def frame_offsets(f):
         return V.tensor_scalar(T.offp[:, K * f:K * f + K], T.n32[:, :], T.pp[:, cd + f:cd + f + 1],
@@ -155,7 +159,7 @@ def rank_program(g, core, T, topo):
             inc(clamp(fr(T.xw, f, f + 1, PAD), T.tmp[:, :]), "done")
             done_at[f] = n["done"]
     else:
-        inc(A.activation(fr(T.bw, 0, WORDS_SCALAR), words(0, WORDS_SCALAR), Copy), "bw0")
+        inc(A.activation(fr(T.bw, WORDS_VECTOR, F), words(WORDS_VECTOR, F), Copy), "bw0")
         for m in range(K):
             inc(V.tensor_scalar(T.t1[:, m::K], T.pp[:, cd:nc], T.n32[:, m:m + 1], None, op.mult), "offp")
         V.wait_ge(sem.offp, n["offp"])
@@ -165,34 +169,35 @@ def rank_program(g, core, T, topo):
         inc(V.tensor_copy(T.offp[:, :], T.t2[:, :]), "offp")
         V.wait_ge(sem.offb, K)
         V.wait_ge(sem.book, 16)
-        inc(V.tensor_copy(fr(T.bw, WORDS_SCALAR, F), words(WORDS_SCALAR, F)), "bwv")
+        inc(V.tensor_copy(fr(T.bw, 0, WORDS_VECTOR), words(0, WORDS_VECTOR)), "bwv")
         V.wait_ge(sem.offp, n["offp"])
-        V.wait_ge(sem.bw0, 1)
         V.wait_ge(sem.bwv, 1)
         A.wait_ge(sem.offp, n["offp"])
-        P.wait_ge(sem.bw0, 1)
         P.wait_ge(sem.bwv, 1)
 
         engines = len(topo.engines(T.cores[r - 1], core))
         pre_at = {}
-        for j in range(len(BATCHES)):
-            A.wait_ge(sem["arr%d" % j], engines)
-            fs = [f for f in range(starts[j], starts[j + 1]) if f not in ON_VECTOR]
-            for k, f in enumerate(fs):
-                if n.get("cp%d" % k):
-                    P.wait_ge(sem["cp%d" % k], n["cp%d" % k])
-                P.matmul(T["ps%d" % k][:, 0:L], T.ident[:, :], fr(T.bw, f, f + 1), True, False)
-            for k in range(len(fs) + 1):
-                if k < len(fs):
-                    f = fs[k]
-                    inc(A.activation(fr(T.lg, f, f + 1), lower(f), Copy, scale=-1.0), "lg%d" % k)
-                    P.wait_ge(sem["lg%d" % k], n["lg%d" % k])
-                    inc(P.matmul(T["ps%d" % k][:, 0:L], T.ident[:, :], fr(T.lg, f, f + 1), False, True), "pe%d" % k)
-                if k > 0:
-                    f = fs[k - 1]
-                    A.wait_ge(sem["pe%d" % (k - 1)], n["pe%d" % (k - 1)])
-                    inc(A.activation(fr(T.pre, f, f + 1), T["ps%d" % (k - 1)][:, 0:L], Copy), "cp%d" % (k - 1))
-                    pre_at[f] = ("cp%d" % (k - 1), n["cp%d" % (k - 1)])
+        fs = [f for f in range(F) if f not in ON_VECTOR]
+        seen = 0
+        for i in range(len(fs) + 1):
+            if i < len(fs):
+                f, k = fs[i], str(i % SLOTS)
+                while seen <= batch_of[f]:
+                    A.wait_ge(sem["arr%d" % seen], engines)
+                    seen += 1
+                if f == WORDS_VECTOR:
+                    P.wait_ge(sem.bw0, 1)
+                if n.get("cp" + k):
+                    P.wait_ge(sem["cp" + k], n["cp" + k])
+                P.matmul(T["ps" + k][:, 0:L], T.ident[:, :], fr(T.bw, f, f + 1), True, False)
+                inc(A.activation(fr(T.lg, f, f + 1), lower(f), Copy, scale=-1.0), "lg" + k)
+                P.wait_ge(sem["lg" + k], n["lg" + k])
+                inc(P.matmul(T["ps" + k][:, 0:L], T.ident[:, :], fr(T.lg, f, f + 1), False, True), "pe" + k)
+            if i > 0:
+                f, k = fs[i - 1], str((i - 1) % SLOTS)
+                A.wait_ge(sem["pe" + k], n["pe" + k])
+                inc(A.activation(fr(T.pre, f, f + 1), T["ps" + k][:, 0:L], Copy), "cp" + k)
+                pre_at[f] = ("cp" + k, n["cp" + k])
 
         seen = 0
         for f in range(F):
@@ -245,8 +250,9 @@ def rank_program(g, core, T, topo):
         A.dma_start(fr(T.y, F - 4, F - 2), fr(T.tail, 0, 2)).then_inc(sem.hst, 16)
         A.wait_ge(sem.done, done_at[F - 2])
         inc(A.activation(fr(T.tail, 2, 3), fr(T.xw, F - 2, F - 1, PAD), Copy), "f32")
-        Y.wait_ge(sem.f32, 2)
+        A.wait_ge(sem.f32, 2)
+        A.dma_start(fr(T.y, F - 2, F - 1), fr(T.tail, 2, 3)).then_inc(sem.hst, 16)
         Y.wait_ge(sem.done, done_at[F - 1])
-        Y.dma_start(fr(T.y, F - 2, F), fr(T.tail, 2, 4)).then_inc(sem.hst, 16)
-        Y.wait_ge(sem.hst, 32)
+        Y.dma_start(fr(T.y, F - 1, F), fr(T.tail, 3, 4)).then_inc(sem.hst, 16)
+        Y.wait_ge(sem.hst, 48)
     g.wait_ge(sem.gst, 16 * stored[1])

@@ -3,23 +3,25 @@ from concourse.mybir import AluOpType, ActivationFunctionType
 F, L, W, S = 32, 128, 16, 4096
 PAD = 16
 K = L // 16
-BATCHES = [1] * 32
-ON_VECTOR = (0, 1)
-WORDS0 = [1, 2, 3, 5, 8, 12, 18, 26, 32]
+SCALE = 16513.0 * 1024
+AHEAD0 = 2
 WORDS_VECTOR = 11
-MID_STORES = {0: {}, 1: {}, 2: {}}
-LAST_STORES = [4, 8, 12, 16, 20, 24, 28]
-SLOTS = 2
+SKEW = 1
+SLOTS = 4
+PIECE = 4
+TAIL = 4
 
 SCRATCH = {
     "bk": ("sbuf", [128, W * L], "bfloat16"),
-    "xw": ("sbuf", [128, PAD + S], "bfloat16"),
+    "xi": ("sbuf", [128, PAD + S], "int32"),
+    "z": ("sbuf", [128, S], "bfloat16"),
     "lw": ("sbuf", [128, PAD + S], "bfloat16"),
     "bw": ("sbuf", [128, S], "bfloat16"),
     "lg": ("sbuf", [128, S], "bfloat16"),
-    "pre": ("sbuf", [128, S], "bfloat16"),
-    "tmp": ("sbuf", [128, L], "bfloat16"),
-    "tail": ("sbuf", [128, 4 * L], "float32"),
+    "pre": ("sbuf", [128, S], "float32"),
+    "yf": ("sbuf", [128, S], "float32"),
+    "tmp": ("sbuf", [128, L], "float32"),
+    "half": ("sbuf", [128, PIECE * L], "float32"),
     "pi": ("sbuf", [128, 5 * F], "int32"),
     "pf": ("sbuf", [128, 5 * F], "float32"),
     "cst": ("sbuf", [128, 5 * F], "float32"),
@@ -43,11 +45,9 @@ SCRATCH = {
 for _k in range(SLOTS):
     SCRATCH["ps%d" % _k] = ("psum", [128, 512], "float32")
 
-SEMAPHORES = (["par", "gpar", "book", "iota", "vi", "convw", "conv", "mmw", "mm", "offb", "offp", "bwv", "low", "own",
-               "done", "sent", "gst", "hst", "f32"]
-              + ["arr%d" % j for j in range(len(BATCHES))]
-              + ["bw%d" % j for j in range(len(WORDS0))]
-              + [n + str(k) for n in ("lg", "pe", "cp") for k in range(SLOTS)])
+SEMAPHORES = (["par", "gpar", "book", "iota", "vi", "convw", "conv", "mmw", "mm", "offb", "offp", "bwv", "bws", "low",
+               "done", "zv", "zs", "sent", "go", "gst", "hst", "fill", "half", "yv", "ys", "lg", "pe", "cp"]
+              + ["arr%d" % j for j in range(F)])
 
 
 def rank_program(g, core, T, topo):
@@ -57,11 +57,17 @@ def rank_program(g, core, T, topo):
     last = r == len(T.cores) - 1
     V, A, P, Y, sem = g.vector, g.scalar, g.tensor, g.sync, T.sem
     op, Copy = AluOpType, ActivationFunctionType.Copy
+    sign = float((-1) ** r)
+    zsign = sign if last else 1.0
     n = {}
 
     def inc(ins, name):
         n[name] = n.get(name, 0) + 1
         ins.then_inc(sem[name], 1)
+        return name, n[name]
+
+    def wait(q, at):
+        q.wait_ge(sem[at[0]], at[1])
 
     def fr(t, f0, f1, pad=0):
         return t[:, pad + L * f0:pad + L * f1]
@@ -70,15 +76,13 @@ def rank_program(g, core, T, topo):
         return T.bk[:, :].indirect(T.offb[:, K * f0:K * f1])
 
     def own(f):
-        return T.xw[:, 0:PAD + L * f].indirect(T.offp[:, K * f:K * f + K])
+        return T.xi[:, 0:PAD + L * f].indirect(T.offp[:, K * f:K * f + K])
 
     def lower(f):
         return T.lw[:, 0:PAD + L * (f + 1)].indirect(T.offp[:, K * (F + f):K * (F + f) + K])
 
     lists = 1 if r == 0 else 2
     ca, cd, nc = F, F + lists * F, F + 2 * lists * F
-    starts = [sum(BATCHES[:j]) for j in range(len(BATCHES) + 1)]
-    batch_of = [j for j, b in enumerate(BATCHES) for _ in range(b)]
 
     par_sem = "gpar" if r >= 2 else "par"
     (g if r >= 2 else Y).dma_start(T.pi[0:8, :], T.par[:, :]).then_inc(sem[par_sem], 16)
@@ -93,9 +97,11 @@ def rank_program(g, core, T, topo):
         inc(g.iota(T.iio[:, :], [[-1, 128]], 0, 1, **fl), "iota")
     inc(V.memset(T.cst[0:1, cd:nc], -32.0 * 64), "vi")
     inc(V.memset(T.w64[0:1, :], 1.0 / 64), "vi")
-    inc(V.memset(T.xw[:, 0:PAD], 0.0), "vi")
+    inc(V.memset(T.xi[:, 0:PAD], 0), "vi")
     if r:
-        inc(V.memset(T.lw[:, 0:PAD], 0.0), "vi")
+        inc(V.memset(T.lw[:, 0:PAD], 0.5), "vi")
+    if last:
+        inc(V.memset(T.half[:, :], -0.5), "half")
     V.wait_ge(sem.iota, n["iota"])
     inc(V.tensor_scalar(T.pq[:, :], T.pa[:, :], 15, None, op.bitwise_and), "vi")
     inc(V.tensor_scalar(T.em[0:8, :], T.eio[0:8, :], 0.0, None, op.is_equal), "vi")
@@ -106,6 +112,12 @@ def rank_program(g, core, T, topo):
     inc(V.tensor_tensor(T.i8[:, :], T.pq[:, :], T.pb[:, :], op.add), "vi")
     V.wait_ge(sem.vi, n["vi"])
     inc(V.tensor_scalar(T.n32[:, :], T.i8[:, :], -1.0 / 32, None, op.mult), "vi")
+
+    if last:
+        Y.wait_ge(sem.half, 1)
+        Y.wait_ge(sem.book, 16)
+        for f in range(0, F - TAIL, PIECE):
+            Y.dma_start(fr(T.y, f, f + PIECE), T.half[:, :]).then_inc(sem.fill, 16)
 
     V.wait_ge(sem[par_sem], 16)
     inc(V.tensor_copy(T.pf[0:8, 0:F], T.pi[0:8, 0:F]), "convw")
@@ -132,34 +144,38 @@ def rank_program(g, core, T, topo):
         return V.tensor_scalar(T.offp[:, K * f:K * f + K], T.n32[:, :], T.pp[:, cd + f:cd + f + 1],
                                T.pp[:, ca + f:ca + f + 1], op.mult, op.subtract)
 
-    def clamp(out, in_):
-        return V.tensor_scalar(out, in_, -127.0, 127.0, op.max, op.min)
+    def chain(f):
+        return V.tensor_tensor(fr(T.xi, f, f + 1, PAD), own(f), fr(T.pre, f, f + 1), op.add)
 
-    done_at = {}
+    z_at = {}
     A.wait_ge(sem.offb, K)
     A.wait_ge(sem.book, 16)
     if r == 0:
         ahead = 4
         for f in range(1, ahead + 1):
             inc(frame_offsets(f), "done")
-        for j in range(len(WORDS0) - 1):
-            inc(A.activation(fr(T.bw, WORDS0[j], WORDS0[j + 1]), words(WORDS0[j], WORDS0[j + 1]), Copy), "bw%d" % j)
         V.wait_ge(sem.offb, K)
         V.wait_ge(sem.book, 16)
-        inc(V.tensor_copy(fr(T.xw, 0, 1, PAD), words(0, 1)), "done")
-        done_at[0] = n["done"]
+        z_at[0] = inc(V.tensor_scalar(fr(T.z, 0, 1), words(0, 1), 0.5, None, op.add), "zv")
+        inc(V.tensor_scalar(fr(T.xi, 0, 1, PAD), words(0, 1), SCALE, None, op.mult), "done")
+        pre_at = {}
+
+        def word(f):
+            pre_at[f] = inc(A.activation(fr(T.pre, f, f + 1), words(f, f + 1), Copy, scale=SCALE), "bws")
+
+        for f in range(1, 1 + AHEAD0):
+            word(f)
         for f in range(1, F):
-            if f in WORDS0:
-                V.wait_ge(sem["bw%d" % WORDS0.index(f)], 1)
+            wait(V, pre_at[f])
             V.wait_ge(sem.done, n["done"])
-            inc(V.tensor_tensor(T.tmp[:, :], own(f), fr(T.bw, f, f + 1), op.add), "own")
+            wait(A, inc(chain(f), "done"))
             if ahead <= f < F - 1:
                 inc(frame_offsets(f + 1), "done")
-            V.wait_ge(sem.own, n["own"])
-            inc(clamp(fr(T.xw, f, f + 1, PAD), T.tmp[:, :]), "done")
-            done_at[f] = n["done"]
+            z_at[f] = inc(A.activation(fr(T.z, f, f + 1), fr(T.xi, f, f + 1, PAD), Copy, bias=0.5, scale=1 / SCALE), "zs")
+            if f + AHEAD0 < F:
+                word(f + AHEAD0)
     else:
-        inc(A.activation(fr(T.bw, WORDS_VECTOR, F), words(WORDS_VECTOR, F), Copy), "bw0")
+        inc(A.activation(fr(T.bw, WORDS_VECTOR, F), words(WORDS_VECTOR, F), Copy, scale=sign), "bws")
         for m in range(K):
             inc(V.tensor_scalar(T.t1[:, m::K], T.pp[:, cd:nc], T.n32[:, m:m + 1], None, op.mult), "offp")
         V.wait_ge(sem.offp, n["offp"])
@@ -169,90 +185,89 @@ def rank_program(g, core, T, topo):
         inc(V.tensor_copy(T.offp[:, :], T.t2[:, :]), "offp")
         V.wait_ge(sem.offb, K)
         V.wait_ge(sem.book, 16)
-        inc(V.tensor_copy(fr(T.bw, 0, WORDS_VECTOR), words(0, WORDS_VECTOR)), "bwv")
+        inc(V.tensor_scalar(fr(T.bw, 0, WORDS_VECTOR), words(0, WORDS_VECTOR), sign, None, op.mult), "bwv")
         V.wait_ge(sem.offp, n["offp"])
         V.wait_ge(sem.bwv, 1)
         A.wait_ge(sem.offp, n["offp"])
         P.wait_ge(sem.bwv, 1)
 
         engines = len(topo.engines(T.cores[r - 1], core))
-        pre_at = {}
-        fs = [f for f in range(F) if f not in ON_VECTOR]
-        seen = 0
-        for i in range(len(fs) + 1):
-            if i < len(fs):
-                f, k = fs[i], str(i % SLOTS)
-                while seen <= batch_of[f]:
-                    A.wait_ge(sem["arr%d" % seen], engines)
-                    seen += 1
+        pre_at, pe_at = {}, {}
+        A.wait_ge(sem.arr0, engines)
+        for f in range(1, F + SKEW):
+            if f < F:
+                bank = T["ps%d" % (f % SLOTS)][:, 0:L]
+                A.wait_ge(sem["arr%d" % f], engines)
                 if f == WORDS_VECTOR:
-                    P.wait_ge(sem.bw0, 1)
-                if n.get("cp" + k):
-                    P.wait_ge(sem["cp" + k], n["cp" + k])
-                P.matmul(T["ps" + k][:, 0:L], T.ident[:, :], fr(T.bw, f, f + 1), True, False)
-                inc(A.activation(fr(T.lg, f, f + 1), lower(f), Copy, scale=-1.0), "lg" + k)
-                P.wait_ge(sem["lg" + k], n["lg" + k])
-                inc(P.matmul(T["ps" + k][:, 0:L], T.ident[:, :], fr(T.lg, f, f + 1), False, True), "pe" + k)
-            if i > 0:
-                f, k = fs[i - 1], str((i - 1) % SLOTS)
-                A.wait_ge(sem["pe" + k], n["pe" + k])
-                inc(A.activation(fr(T.pre, f, f + 1), T["ps" + k][:, 0:L], Copy), "cp" + k)
-                pre_at[f] = ("cp" + k, n["cp" + k])
+                    P.wait_ge(sem.bws, 1)
+                if f - SLOTS in pre_at:
+                    wait(P, pre_at[f - SLOTS])
+                P.matmul(bank, T.ident[:, :], fr(T.bw, f, f + 1), True, False)
+                wait(P, inc(A.activation(fr(T.lg, f, f + 1), lower(f), Copy), "lg"))
+                pe_at[f] = inc(P.matmul(bank, T.ident[:, :], fr(T.lg, f, f + 1), False, True), "pe")
+            h = f - SKEW
+            if h >= 1:
+                wait(A, pe_at[h])
+                pre_at[h] = inc(A.activation(fr(T.pre, h, h + 1), T["ps%d" % (h % SLOTS)][:, 0:L], Copy,
+                                             bias=-0.5 * SCALE, scale=SCALE), "cp")
 
-        seen = 0
-        for f in range(F):
-            out = fr(T.xw, f, f + 1, PAD)
-            if last and f == F - 1:
-                out = fr(T.tail, 3, 4)
-            if f in ON_VECTOR:
-                while seen <= batch_of[f]:
-                    V.wait_ge(sem["arr%d" % seen], engines)
-                    seen += 1
-                inc(V.tensor_tensor(fr(T.pre, f, f + 1), lower(f), fr(T.bw, f, f + 1), op.subtract), "low")
-                pre_at[f] = ("low", n["low"])
-            if f:
-                V.wait_ge(sem.done, n["done"])
-            V.wait_ge(sem[pre_at[f][0]], pre_at[f][1])
-            if f == 0:
-                inc(V.tensor_scalar(T.tmp[:, :], fr(T.pre, 0, 1), -1.0 if 0 in ON_VECTOR else 1.0, None, op.mult), "own")
-            else:
-                inc(V.tensor_tensor(T.tmp[:, :], own(f), fr(T.pre, f, f + 1),
-                                    op.subtract if f in ON_VECTOR else op.add), "own")
-            V.wait_ge(sem.own, n["own"])
-            inc(clamp(out, T.tmp[:, :]), "done")
-            done_at[f] = n["done"]
+        def clean(f):
+            z_at[f] = inc(V.tensor_scalar(fr(T.z, f, f + 1), fr(T.xi, f, f + 1, PAD), zsign / SCALE, 0.5,
+                                          op.mult, op.add), "zv")
 
-    stored = [0, 0]
+        V.wait_ge(sem.arr0, engines)
+        wait(V, inc(V.tensor_tensor(T.tmp[:, :], lower(0), fr(T.bw, 0, 1), op.add), "low"))
+        if not last:
+            z_at[0] = inc(V.tensor_scalar(fr(T.z, 0, 1), T.tmp[:, :], -126.5, 127.5, op.max, op.min), "zv")
+        inc(V.tensor_scalar(fr(T.xi, 0, 1, PAD), T.tmp[:, :], 0.5, SCALE, op.subtract, op.mult), "done")
+        for f in range(1, F):
+            V.wait_ge(sem.done, n["done"])
+            wait(V, pre_at[f])
+            inc(chain(f), "done")
+            if f - 1 not in z_at:
+                clean(f - 1)
+        V.wait_ge(sem.done, n["done"])
+        clean(F - 1)
 
-    def store(f1):
-        g.dma_start(fr(T.y, stored[0], f1), fr(T.xw, stored[0], f1, PAD)).then_inc(sem.gst, 16)
-        stored[0], stored[1] = f1, stored[1] + 1
+    ysign = 1.0 if last else sign
+
+    def whole_v(f0, f1):
+        wait(V, z_at[f1 - 1])
+        return inc(V.tensor_scalar(fr(T.yf, f0, f1), fr(T.z, f0, f1), 0.5, ysign, op.subtract, op.mult), "yv")
+
+    def whole_s(f0, f1):
+        wait(A, z_at[f1 - 1])
+        return inc(A.activation(fr(T.yf, f0, f1), fr(T.z, f0, f1), Copy, bias=-0.5 * ysign, scale=ysign), "ys")
+
+    stores = [0]
+
+    def store(q, f0, f1, at):
+        wait(q, at)
+        q.dma_start(fr(T.y, f0, f1), fr(T.yf, f0, f1)).then_inc(sem.hst, 16)
+        stores[0] += 1
 
     if not last:
         dst = T.cores[r + 1]
         rid, pid, _ = topo.addr(dst)
         mask = topo.mask(core, dst)
-        for j in range(len(BATCHES)):
-            g.wait_ge(sem.done, done_at[starts[j + 1] - 1])
-            g.remote_dma(fr(T.lw, starts[j], starts[j + 1], PAD), fr(T.xw, starts[j], starts[j + 1], PAD),
-                         sem["arr%d" % j], sem.sent, pid, rid, mask)
-            if j in MID_STORES[r]:
-                store(MID_STORES[r][j])
-        store(F)
-        g.wait_ge(sem.sent, len(BATCHES) * len(topo.engines(core, dst)))
+        for f in range(F):
+            wait(g, z_at[f])
+            g.remote_dma(fr(T.lw, f, f + 1, PAD), fr(T.z, f, f + 1), sem["arr%d" % f], sem.sent, pid, rid, mask)
+        g.sem_inc(sem.go, 1)
+        if r == 0:
+            wait(V, z_at[F - 1])
+            wait(A, z_at[0])
+        Y.wait_ge(sem.go, 1)
+        for j, f in enumerate(range(0, F, PIECE)):
+            store(Y, f, f + PIECE, (whole_v if j % 2 else whole_s)(f, f + PIECE))
+        g.wait_ge(sem.sent, F * len(topo.engines(core, dst)))
     else:
-        for f1 in LAST_STORES:
-            g.wait_ge(sem.done, done_at[f1 - 1])
-            store(f1)
-        A.wait_ge(sem.done, done_at[F - 3])
-        inc(A.activation(fr(T.tail, 0, 2), fr(T.xw, F - 4, F - 2, PAD), Copy), "f32")
-        A.wait_ge(sem.f32, 1)
-        A.dma_start(fr(T.y, F - 4, F - 2), fr(T.tail, 0, 2)).then_inc(sem.hst, 16)
-        A.wait_ge(sem.done, done_at[F - 2])
-        inc(A.activation(fr(T.tail, 2, 3), fr(T.xw, F - 2, F - 1, PAD), Copy), "f32")
-        A.wait_ge(sem.f32, 2)
-        A.dma_start(fr(T.y, F - 2, F - 1), fr(T.tail, 2, 3)).then_inc(sem.hst, 16)
-        Y.wait_ge(sem.done, done_at[F - 1])
-        Y.dma_start(fr(T.y, F - 1, F), fr(T.tail, 3, 4)).then_inc(sem.hst, 16)
-        Y.wait_ge(sem.hst, 48)
-    g.wait_ge(sem.gst, 16 * stored[1])
+        g.wait_ge(sem.fill, 16 * ((F - TAIL) // PIECE))
+        for f in range(0, F - TAIL, PIECE):
+            wait(g, z_at[f + PIECE - 1])
+            g.dma_start(fr(T.y, f, f + PIECE), fr(T.z, f, f + PIECE), accum_op=op.add).then_inc(sem.gst, 16)
+        store(A, F - 4, F - 2, whole_s(F - 4, F - 2))
+        store(A, F - 2, F - 1, whole_s(F - 2, F - 1))
+        store(Y, F - 1, F, whole_v(F - 1, F))
+        g.wait_ge(sem.gst, 16 * ((F - TAIL) // PIECE))
+    Y.wait_ge(sem.hst, 16 * stores[0])

@@ -3,13 +3,21 @@ from concourse.mybir import AluOpType, ActivationFunctionType
 F, L, W, S = 32, 128, 16, 4096
 PAD = 16
 K = L // 16
-SCALE = 16513.0 * 1024
-AHEAD0 = 2
-WORDS_VECTOR = 11
-SKEW = 1
-SLOTS = 4
+SCALES = (16384.0 * 1024, 129.0 * 1024)
+SCALE = sum(SCALES)
+ROWS = 48
+GLIDES, LAGS = slice(0, 8), slice(32, 40)
+LH_VECTOR = 3
+MID = 2048
+FIRST = 8
+QUICK = 2
+AHEAD0 = 3
+BANK = 4
+BANKS_VECTOR = 4
+LATE_VECTOR, LATE_SCALAR = 2, 1
+LEAD_PRE, LEAD_LOW = 2, 4
 PIECE = 4
-TAIL = 4
+ADDED = 28
 
 SCRATCH = {
     "bk": ("sbuf", [128, W * L], "bfloat16"),
@@ -17,36 +25,29 @@ SCRATCH = {
     "z": ("sbuf", [128, S], "bfloat16"),
     "lw": ("sbuf", [128, PAD + S], "bfloat16"),
     "bw": ("sbuf", [128, S], "bfloat16"),
-    "lg": ("sbuf", [128, S], "bfloat16"),
+    "lg": ("sbuf", [128, S], "float32"),
     "pre": ("sbuf", [128, S], "float32"),
     "yf": ("sbuf", [128, S], "float32"),
     "tmp": ("sbuf", [128, L], "float32"),
     "half": ("sbuf", [128, PIECE * L], "float32"),
     "pi": ("sbuf", [128, 5 * F], "int32"),
-    "pf": ("sbuf", [128, 5 * F], "float32"),
-    "cst": ("sbuf", [128, 5 * F], "float32"),
-    "w64": ("sbuf", [128, 128], "float32"),
-    "eio": ("sbuf", [128, 128], "float32"),
-    "em": ("sbuf", [128, 128], "float32"),
+    "pat": ("sbuf", [128, 128], "int32"),
+    "msk": ("sbuf", [128, 128], "int32"),
+    "step": ("sbuf", [128, K], "float32"),
+    "col": ("sbuf", [128, K], "float32"),
+    "cf": ("sbuf", [128, 3 * F], "float32"),
+    "rhs": ("sbuf", [128, 3 * F], "float16"),
+    "lh": ("sbuf", [128, K * 128], "bfloat16"),
     "iio": ("sbuf", [128, 128], "float32"),
-    "ident": ("sbuf", [128, 128], "bfloat16"),
-    "pa": ("sbuf", [128, K], "int32"),
-    "pq": ("sbuf", [128, K], "int32"),
-    "pb": ("sbuf", [128, K], "float32"),
-    "i8": ("sbuf", [128, K], "float32"),
-    "n32": ("sbuf", [128, K], "float32"),
-    "t1": ("sbuf", [128, 2 * F * K], "float32"),
-    "t2": ("sbuf", [128, 2 * F * K], "float32"),
+    "ident": ("sbuf", [128, 2 * 128], "bfloat16"),
     "offb": ("sbuf", [128, F * K], "uint16"),
     "offp": ("sbuf", [128, 2 * F * K], "uint16"),
-    "pp": ("psum", [128, 512], "float32"),
-    "pw": ("psum", [128, 512], "float32"),
 }
-for _k in range(SLOTS):
-    SCRATCH["ps%d" % _k] = ("psum", [128, 512], "float32")
+for _k in range(F // BANK):
+    SCRATCH["ps%d" % _k] = ("psum", [128, BANK * L], "float32")
 
-SEMAPHORES = (["par", "gpar", "book", "iota", "vi", "convw", "conv", "mmw", "mm", "offb", "offp", "bwv", "bws", "low",
-               "done", "zv", "zs", "sent", "go", "gst", "hst", "fill", "half", "yv", "ys", "lg", "pe", "cp"]
+SEMAPHORES = (["par", "par2", "book", "iota", "vi", "lhv", "lhs", "conv", "mm", "off", "bwv", "bws", "low", "pre",
+               "done", "zv", "zs", "sent", "go", "gst", "hst", "fill", "half", "yv", "ys", "lg", "pe"]
               + ["arr%d" % j for j in range(F)])
 
 
@@ -56,9 +57,10 @@ def rank_program(g, core, T, topo):
         return
     last = r == len(T.cores) - 1
     V, A, P, Y, sem = g.vector, g.scalar, g.tensor, g.sync, T.sem
-    op, Copy = AluOpType, ActivationFunctionType.Copy
+    op, Copy, Relu = AluOpType, ActivationFunctionType.Copy, ActivationFunctionType.Relu
     sign = float((-1) ** r)
     zsign = sign if last else 1.0
+    pw, pp = T.ps6, T.ps7
     n = {}
 
     def inc(ins, name):
@@ -82,152 +84,207 @@ def rank_program(g, core, T, topo):
         return T.lw[:, 0:PAD + L * (f + 1)].indirect(T.offp[:, K * (F + f):K * (F + f) + K])
 
     lists = 1 if r == 0 else 2
-    ca, cd, nc = F, F + lists * F, F + 2 * lists * F
 
-    par_sem = "gpar" if r >= 2 else "par"
-    (g if r >= 2 else Y).dma_start(T.pi[0:8, :], T.par[:, :]).then_inc(sem[par_sem], 16)
+    Y.dma_start(T.pi[LAGS, :], T.par[:, :]).then_inc(sem.par, 16)
+    (g if last else A).dma_start(T.pi[GLIDES, :], T.par[:, :]).then_inc(sem.par2, 16)
     Y.dma_start(T.bk[:, :], T.book[:, :]).then_inc(sem.book, 16)
 
     fl = {"allow_small_or_imprecise_dtypes": True}
-    inc(g.iota(T.eio[0:8, :], [[1, 8], [0, 16]], 0, -1, **fl), "iota")
-    inc(g.iota(T.cst[0:1, ca:cd], [[0, lists], [-64 * L, F]], -(64 * PAD + 31), 0, **fl), "iota")
-    inc(g.iota(T.pa[:, :], [[0, K]], 0, 1), "iota")
-    inc(g.iota(T.pb[:, :], [[16, K]], 0, 0, **fl), "iota")
+    R, UP, DOWN = slice(0, ROWS), slice(0, 32), slice(32, ROWS)
+    pat = inc(g.iota(T.pat[R, :], [[-1024, 8], [1, 16]], 31 * 1024, 1024), "iota")
+    step = inc(g.iota(T.step[UP, :], [[16, K]], -31 * 1024, 0, **fl), "iota")
+    frames = inc(g.iota(T.cf[R, F:(1 + lists) * F], [[0, lists], [L, F]], -MID, 0, **fl), "iota")
     if r:
-        inc(g.iota(T.iio[:, :], [[-1, 128]], 0, 1, **fl), "iota")
-    inc(V.memset(T.cst[0:1, cd:nc], -32.0 * 64), "vi")
-    inc(V.memset(T.w64[0:1, :], 1.0 / 64), "vi")
+        ident = inc(g.iota(T.iio[:, :], [[-1, 128]], 0, 1, **fl), "iota")
+    else:
+        cols = inc(g.iota(T.col[:, :], [[32 * 16, K]], 0, 0, **fl), "iota")
+    inc(V.memset(T.step[DOWN, :], 32.0 - 7 * 1024), "vi")
+    inc(V.memset(T.cf[UP, 0:F], 32.0), "vi")
+    filled = inc(V.memset(T.cf[DOWN, 0:F], -float(MID)), "vi")
     inc(V.memset(T.xi[:, 0:PAD], 0), "vi")
     if r:
         inc(V.memset(T.lw[:, 0:PAD], 0.5), "vi")
-    if last:
-        inc(V.memset(T.half[:, :], -0.5), "half")
-    V.wait_ge(sem.iota, n["iota"])
-    inc(V.tensor_scalar(T.pq[:, :], T.pa[:, :], 15, None, op.bitwise_and), "vi")
-    inc(V.tensor_scalar(T.em[0:8, :], T.eio[0:8, :], 0.0, None, op.is_equal), "vi")
-    if r:
-        inc(V.tensor_scalar(T.ident[:, :], T.iio[:, :], 0.0, None, op.is_equal), "vi")
-    V.wait_ge(sem.vi, n["vi"])
-    made = n["vi"]
-    inc(V.tensor_tensor(T.i8[:, :], T.pq[:, :], T.pb[:, :], op.add), "vi")
-    V.wait_ge(sem.vi, n["vi"])
-    inc(V.tensor_scalar(T.n32[:, :], T.i8[:, :], -1.0 / 32, None, op.mult), "vi")
-
-    if last:
-        Y.wait_ge(sem.half, 1)
-        Y.wait_ge(sem.book, 16)
-        for f in range(0, F - TAIL, PIECE):
-            Y.dma_start(fr(T.y, f, f + PIECE), T.half[:, :]).then_inc(sem.fill, 16)
-
-    V.wait_ge(sem[par_sem], 16)
-    inc(V.tensor_copy(T.pf[0:8, 0:F], T.pi[0:8, 0:F]), "convw")
-    if r == 0:
-        moves = [(F, F, 2 * F)]
-    else:
-        moves = [(F, F, F), (2 * F, 3 * F, F), (3 * F, 2 * F, F), (4 * F, 4 * F, F)]
-    for to, frm, w in moves:
-        inc(V.tensor_copy(T.pf[0:8, to:to + w], T.pi[0:8, frm:frm + w]), "conv")
-    P.wait_ge(sem.vi, made)
-    P.matmul(T.pp[:, ca:nc], T.w64[0:1, :], T.cst[0:1, ca:nc], True, False)
-    P.wait_ge(sem.convw, 1)
-    inc(P.matmul(T.pw[:, 0:F], T.em[0:8, :], T.pf[0:8, 0:F], True, True), "mmw")
-    P.wait_ge(sem.conv, n["conv"])
-    inc(P.matmul(T.pp[:, ca:nc], T.em[0:8, :], T.pf[0:8, ca:nc], False, True), "mm")
-
-    V.wait_ge(sem.vi, n["vi"])
-    V.wait_ge(sem.mmw, 1)
+    wait(V, pat)
+    inc(V.tensor_scalar(T.msk[UP, :], T.pat[UP, :], 31 * 1024 + 15, None, op.bitwise_and), "vi")
+    masked = inc(V.tensor_scalar(T.msk[DOWN, :], T.pat[DOWN, :], 7 * 1024, None, op.bitwise_and), "vi")
+    wait(V, frames)
+    wait(V, filled)
+    copied = inc(V.tensor_copy(T.rhs[R, 0:(1 + lists) * F], T.cf[R, 0:(1 + lists) * F]), "vi")
+    for q in (V, A):
+        wait(q, masked)
+        wait(q, step)
+    lh_at = {}
     for m in range(K):
-        inc(V.tensor_scalar(T.offb[:, m::K], T.pw[:, 0:F], float(L), T.i8[:, m:m + 1], op.mult, op.add), "offb")
-    V.wait_ge(sem.mm, 1)
+        out = T.lh[R, 128 * m:128 * m + 128]
+        if m < LH_VECTOR:
+            lh_at[m] = inc(V.tensor_scalar(out, T.msk[R, :], T.step[R, m:m + 1], 0.0, op.add, op.max), "lhv")
+        else:
+            lh_at[m] = inc(A.activation(out, T.msk[R, :], Relu, bias=T.step[R, m:m + 1]), "lhs")
+    wait(V, copied)
 
-    def frame_offsets(f):
-        return V.tensor_scalar(T.offp[:, K * f:K * f + K], T.n32[:, :], T.pp[:, cd + f:cd + f + 1],
-                               T.pp[:, ca + f:ca + f + 1], op.mult, op.subtract)
+    V.wait_ge(sem.par, 16)
+    conv_w = inc(V.tensor_scalar(T.rhs[LAGS, 0:F], T.pi[LAGS, 0:F], float(L), float(MID), op.mult, op.add), "conv")
+    for j in range(lists):
+        for rows, table, less in ((LAGS, 1 + 2 * j, MID), (GLIDES, 2 + 2 * j, 32)):
+            if rows == GLIDES:
+                V.wait_ge(sem.par2, 16)
+            conv_p = inc(V.tensor_scalar(T.rhs[rows, (1 + j) * F:(2 + j) * F], T.pi[rows, table * F:(table + 1) * F],
+                                         float(less), -1.0, op.subtract, op.mult), "conv")
+
+    def spread(bank, c0, c1):
+        for m in range(K):
+            if m in lh_at:
+                wait(P, lh_at.pop(m))
+            ins = P.matmul(bank[:, m:K * (c1 - c0):K], T.lh[R, 128 * m:128 * m + 128], T.rhs[R, c0:c1], True, True)
+        return inc(ins, "mm")
+
+    def cast_words(f0, f1):
+        return inc(V.tensor_scalar(T.offb[:, K * f0:K * f1], pw[:, K * f0:K * f1], 1 / 32, None, op.mult), "off")
+
+    def cast_places(bank, at, c0, c1):
+        return inc(V.tensor_scalar(T.offp[:, c0:c1], bank[:, at + c0:at + c1], 1 / 32, PAD + 31 / 64,
+                                   op.mult, op.add), "off")
 
     def chain(f):
-        return V.tensor_tensor(fr(T.xi, f, f + 1, PAD), own(f), fr(T.pre, f, f + 1), op.add)
+        return inc(V.tensor_tensor(fr(T.xi, f, f + 1, PAD), own(f), fr(T.pre, f, f + 1), op.add), "done")
 
-    z_at = {}
-    A.wait_ge(sem.offb, K)
+    x_at, z_at = {}, {}
+
+    def clean(f):
+        wait(A, x_at[f])
+        z_at[f] = inc(A.activation(fr(T.z, f, f + 1), fr(T.xi, f, f + 1, PAD), Copy, bias=0.5, scale=zsign / SCALE), "zs")
+
     A.wait_ge(sem.book, 16)
     if r == 0:
-        ahead = 4
-        for f in range(1, ahead + 1):
-            inc(frame_offsets(f), "done")
-        V.wait_ge(sem.offb, K)
+        wait(P, conv_w)
+        wait(P, lh_at[0])
+        wait(V, inc(P.matmul(T.ps0[:, 0:QUICK], T.lh[R, 0:128], T.rhs[R, 0:QUICK], True, True), "mm"))
+        wait(P, conv_p)
+        spread_p = spread(pw, 0, 2 * F)
+        wait(V, cols)
+        quick = [inc(V.tensor_scalar(T.offb[:, K * f:K * f + K], T.col[:, :], T.ps0[:, f:f + 1], 1 / 32,
+                                     op.add, op.mult), "off") for f in range(QUICK)]
+        wait(V, quick[0])
+        wait(A, quick[0])
         V.wait_ge(sem.book, 16)
-        z_at[0] = inc(V.tensor_scalar(fr(T.z, 0, 1), words(0, 1), 0.5, None, op.add), "zv")
-        inc(V.tensor_scalar(fr(T.xi, 0, 1, PAD), words(0, 1), SCALE, None, op.mult), "done")
-        pre_at = {}
+        x_at[0] = inc(V.tensor_scalar(fr(T.xi, 0, 1, PAD), words(0, 1), SCALE, None, op.mult), "done")
+        z_at[0] = inc(A.activation(fr(T.z, 0, 1), words(0, 1), Copy, bias=0.5), "zs")
+        wait(V, spread_p)
+        pre_at, cast_at = {}, {("w", f): quick[f] for f in range(1, QUICK)}
+        cast_at["p", 1] = cast_places(pw, K * F, K, K * FIRST)
+        cast_at["w", QUICK] = cast_words(QUICK, FIRST)
+        more = [FIRST, (FIRST + F) // 2, F]
 
         def word(f):
+            if ("w", f) in cast_at:
+                wait(A, cast_at["w", f])
             pre_at[f] = inc(A.activation(fr(T.pre, f, f + 1), words(f, f + 1), Copy, scale=SCALE), "bws")
 
         for f in range(1, 1 + AHEAD0):
             word(f)
         for f in range(1, F):
+            if ("p", f) in cast_at:
+                wait(V, cast_at["p", f])
             wait(V, pre_at[f])
-            V.wait_ge(sem.done, n["done"])
-            wait(A, inc(chain(f), "done"))
-            if ahead <= f < F - 1:
-                inc(frame_offsets(f + 1), "done")
-            z_at[f] = inc(A.activation(fr(T.z, f, f + 1), fr(T.xi, f, f + 1, PAD), Copy, bias=0.5, scale=1 / SCALE), "zs")
+            wait(V, x_at[f - 1])
+            x_at[f] = chain(f)
+            if f <= 2 * (len(more) - 1):
+                f0, f1 = more[(f - 1) // 2:(f - 1) // 2 + 2]
+                if f % 2:
+                    cast_at["w", f0] = cast_words(f0, f1)
+                else:
+                    cast_at["p", f0] = cast_places(pw, K * F, K * f0, K * f1)
+            clean(f)
             if f + AHEAD0 < F:
                 word(f + AHEAD0)
     else:
-        inc(A.activation(fr(T.bw, WORDS_VECTOR, F), words(WORDS_VECTOR, F), Copy, scale=sign), "bws")
-        for m in range(K):
-            inc(V.tensor_scalar(T.t1[:, m::K], T.pp[:, cd:nc], T.n32[:, m:m + 1], None, op.mult), "offp")
-        V.wait_ge(sem.offp, n["offp"])
-        for m in range(K):
-            inc(V.tensor_tensor(T.t2[:, m::K], T.t1[:, m::K], T.pp[:, ca:cd], op.subtract), "offp")
-        V.wait_ge(sem.offp, n["offp"])
-        inc(V.tensor_copy(T.offp[:, :], T.t2[:, :]), "offp")
-        V.wait_ge(sem.offb, K)
+        late_v, late_s = (LATE_VECTOR, LATE_SCALAR) if r == 1 else (0, 0)
+        early = F - late_v - late_s
+
+        def words_v(f0, f1):
+            return inc(V.tensor_scalar(fr(T.bw, f0, f1), words(f0, f1), sign, None, op.mult), "bwv")
+
+        def words_s(f0, f1):
+            return inc(A.activation(fr(T.bw, f0, f1), words(f0, f1), Copy, scale=sign), "bws")
+
+        wait(P, conv_w)
+        spread_w = spread(pw, 0, F)
+        wait(P, conv_p)
+        spread_p = spread(pp, F, 3 * F)
+        wait(V, spread_w)
+        offb = cast_words(0, F)
+        wait(V, spread_p)
+        offp = cast_places(pp, 0, 0, 2 * K * F)
+        wait(V, ident)
+        for j, part in enumerate(SCALES):
+            scaled = inc(V.tensor_scalar(T.ident[:, 128 * j:128 * j + 128], T.iio[:, :], 0.0, part,
+                                         op.is_equal, op.mult), "vi")
+        if last:
+            wait(Y, inc(V.memset(T.half[:, :], -0.5), "half"))
+            Y.wait_ge(sem.book, 16)
+            for f in range(0, ADDED, PIECE):
+                Y.dma_start(fr(T.y, f, f + PIECE), T.half[:, :]).then_inc(sem.fill, 16)
+        wait(A, offb)
+        wait(V, offb)
         V.wait_ge(sem.book, 16)
-        inc(V.tensor_scalar(fr(T.bw, 0, WORDS_VECTOR), words(0, WORDS_VECTOR), sign, None, op.mult), "bwv")
-        V.wait_ge(sem.offp, n["offp"])
-        V.wait_ge(sem.bwv, 1)
-        A.wait_ge(sem.offp, n["offp"])
-        P.wait_ge(sem.bwv, 1)
+        word_at = {}
+        for b in range(F // BANK):
+            word_at[b] = [(words_v if b < BANKS_VECTOR else words_s)(BANK * b, min(BANK * b + BANK, early))]
+        wait(V, offp)
+        wait(V, word_at[0][0])
+        wait(A, offp)
 
         engines = len(topo.engines(T.cores[r - 1], core))
-        pre_at, pe_at = {}, {}
-        A.wait_ge(sem.arr0, engines)
-        for f in range(1, F + SKEW):
-            if f < F:
-                bank = T["ps%d" % (f % SLOTS)][:, 0:L]
-                A.wait_ge(sem["arr%d" % f], engines)
-                if f == WORDS_VECTOR:
-                    P.wait_ge(sem.bws, 1)
-                if f - SLOTS in pre_at:
-                    wait(P, pre_at[f - SLOTS])
-                P.matmul(bank, T.ident[:, :], fr(T.bw, f, f + 1), True, False)
-                wait(P, inc(A.activation(fr(T.lg, f, f + 1), lower(f), Copy), "lg"))
-                pe_at[f] = inc(P.matmul(bank, T.ident[:, :], fr(T.lg, f, f + 1), False, True), "pe")
-            h = f - SKEW
-            if h >= 1:
-                wait(A, pe_at[h])
-                pre_at[h] = inc(A.activation(fr(T.pre, h, h + 1), T["ps%d" % (h % SLOTS)][:, 0:L], Copy,
-                                             bias=-0.5 * SCALE, scale=SCALE), "cp")
-
-        def clean(f):
-            z_at[f] = inc(V.tensor_scalar(fr(T.z, f, f + 1), fr(T.xi, f, f + 1, PAD), zsign / SCALE, 0.5,
-                                          op.mult, op.add), "zv")
-
         V.wait_ge(sem.arr0, engines)
         wait(V, inc(V.tensor_tensor(T.tmp[:, :], lower(0), fr(T.bw, 0, 1), op.add), "low"))
         if not last:
             z_at[0] = inc(V.tensor_scalar(fr(T.z, 0, 1), T.tmp[:, :], -126.5, 127.5, op.max, op.min), "zv")
-        inc(V.tensor_scalar(fr(T.xi, 0, 1, PAD), T.tmp[:, :], 0.5, SCALE, op.subtract, op.mult), "done")
+        x_at[0] = inc(V.tensor_scalar(fr(T.xi, 0, 1, PAD), T.tmp[:, :], 0.5, SCALE, op.subtract, op.mult), "done")
+        if late_v:
+            word_at[F // BANK - 1].append(words_v(early, early + late_v))
+
+        lg_at, pre_at, bank_at = {}, {}, {}
+
+        def low(f):
+            A.wait_ge(sem["arr%d" % f], engines)
+            lg_at[f] = inc(A.activation(fr(T.lg, f, f + 1), lower(f), Copy, bias=-0.5 * SCALE, scale=SCALE), "lg")
+
+        def pre(f):
+            if f == 1 or f % BANK == 0:
+                wait(V, bank_at[f // BANK])
+            wait(V, lg_at[f])
+            pre_at[f] = inc(V.tensor_tensor(fr(T.pre, f, f + 1), fr(T.lg, f, f + 1),
+                                            fr(T["ps%d" % (f // BANK)], f % BANK, f % BANK + 1), op.add), "pre")
+
+        A.wait_ge(sem.arr0, engines)
+        for f in range(1, LEAD_LOW + 1):
+            low(f)
+            if f == 2 and late_s:
+                word_at[F // BANK - 1].append(words_s(F - late_s, F))
+
+        wait(P, scaled)
+        wait(P, offp)
+        for b in range(F // BANK):
+            for at in word_at[b]:
+                wait(P, at)
+            for j in range(len(SCALES)):
+                ins = P.matmul(T["ps%d" % b][:, :], T.ident[:, 128 * j:128 * j + 128], fr(T.bw, BANK * b, BANK * b + BANK),
+                               j == 0, j == len(SCALES) - 1)
+            bank_at[b] = inc(ins, "pe")
+
+        for f in range(1, LEAD_PRE + 1):
+            pre(f)
+        if last:
+            clean(0)
         for f in range(1, F):
-            V.wait_ge(sem.done, n["done"])
+            wait(V, x_at[f - 1])
             wait(V, pre_at[f])
-            inc(chain(f), "done")
-            if f - 1 not in z_at:
-                clean(f - 1)
-        V.wait_ge(sem.done, n["done"])
-        clean(F - 1)
+            x_at[f] = chain(f)
+            if f + LEAD_PRE < F:
+                pre(f + LEAD_PRE)
+            clean(f)
+            if f + LEAD_LOW < F:
+                low(f + LEAD_LOW)
 
     ysign = 1.0 if last else sign
 
@@ -254,20 +311,18 @@ def rank_program(g, core, T, topo):
             wait(g, z_at[f])
             g.remote_dma(fr(T.lw, f, f + 1, PAD), fr(T.z, f, f + 1), sem["arr%d" % f], sem.sent, pid, rid, mask)
         g.sem_inc(sem.go, 1)
-        if r == 0:
-            wait(V, z_at[F - 1])
-            wait(A, z_at[0])
+        wait(V, z_at[0])
+        wait(A, z_at[0])
         Y.wait_ge(sem.go, 1)
         for j, f in enumerate(range(0, F, PIECE)):
-            store(Y, f, f + PIECE, (whole_v if j % 2 else whole_s)(f, f + PIECE))
+            store(Y, f, f + PIECE, (whole_s if j % 2 else whole_v)(f, f + PIECE))
         g.wait_ge(sem.sent, F * len(topo.engines(core, dst)))
     else:
-        g.wait_ge(sem.fill, 16 * ((F - TAIL) // PIECE))
-        for f in range(0, F - TAIL, PIECE):
+        g.wait_ge(sem.fill, 16 * (ADDED // PIECE))
+        for f in range(0, ADDED, PIECE):
             wait(g, z_at[f + PIECE - 1])
             g.dma_start(fr(T.y, f, f + PIECE), fr(T.z, f, f + PIECE), accum_op=op.add).then_inc(sem.gst, 16)
-        store(A, F - 4, F - 2, whole_s(F - 4, F - 2))
-        store(A, F - 2, F - 1, whole_s(F - 2, F - 1))
-        store(Y, F - 1, F, whole_v(F - 1, F))
-        g.wait_ge(sem.gst, 16 * ((F - TAIL) // PIECE))
+        for f0, f1 in ((ADDED, F - 2), (F - 2, F - 1), (F - 1, F)):
+            store(Y, f0, f1, whole_v(f0, f1))
+        g.wait_ge(sem.gst, 16 * (ADDED // PIECE))
     Y.wait_ge(sem.hst, 16 * stores[0])

from concourse.mybir import AluOpType, ActivationFunctionType

F, L, W, S = 32, 128, 16, 4096
PAD = 16
K = L // 16
SCALES = (16384.0 * 1024, 129.0 * 1024)
SCALE = sum(SCALES)
ROWS = 48
GLIDES, LAGS = slice(0, 8), slice(32, 40)
LH_VECTOR = 3
MID = 2048
FIRST = 8
QUICK = 2
AHEAD0 = 3
BANK = 4
BANKS_VECTOR = 4
LATE_VECTOR, LATE_SCALAR = 2, 1
LEAD_PRE, LEAD_LOW = 2, 4
PIECE = 4
ADDED = 28

SCRATCH = {
    "bk": ("sbuf", [128, W * L], "bfloat16"),
    "xi": ("sbuf", [128, PAD + S], "int32"),
    "z": ("sbuf", [128, S], "bfloat16"),
    "lw": ("sbuf", [128, PAD + S], "bfloat16"),
    "bw": ("sbuf", [128, S], "bfloat16"),
    "lg": ("sbuf", [128, S], "float32"),
    "pre": ("sbuf", [128, S], "float32"),
    "yf": ("sbuf", [128, S], "float32"),
    "tmp": ("sbuf", [128, L], "float32"),
    "half": ("sbuf", [128, PIECE * L], "float32"),
    "pi": ("sbuf", [128, 5 * F], "int32"),
    "pat": ("sbuf", [128, 128], "int32"),
    "msk": ("sbuf", [128, 128], "int32"),
    "step": ("sbuf", [128, K], "float32"),
    "col": ("sbuf", [128, K], "float32"),
    "cf": ("sbuf", [128, 3 * F], "float32"),
    "rhs": ("sbuf", [128, 3 * F], "float16"),
    "lh": ("sbuf", [128, K * 128], "bfloat16"),
    "iio": ("sbuf", [128, 128], "float32"),
    "ident": ("sbuf", [128, 2 * 128], "bfloat16"),
    "offb": ("sbuf", [128, F * K], "uint16"),
    "offp": ("sbuf", [128, 2 * F * K], "uint16"),
}
for _k in range(F // BANK):
    SCRATCH["ps%d" % _k] = ("psum", [128, BANK * L], "float32")

SEMAPHORES = (["par", "par2", "book", "iota", "vi", "lhv", "lhs", "conv", "mm", "off", "bwv", "bws", "low", "pre",
               "done", "zv", "zs", "sent", "go", "gst", "hst", "fill", "half", "yv", "ys", "lg", "pe"]
              + ["arr%d" % j for j in range(F)])


def rank_program(g, core, T, topo):
    r = T.rank_of(core)
    if r is None:
        return
    last = r == len(T.cores) - 1
    V, A, P, Y, sem = g.vector, g.scalar, g.tensor, g.sync, T.sem
    op, Copy, Relu = AluOpType, ActivationFunctionType.Copy, ActivationFunctionType.Relu
    sign = float((-1) ** r)
    zsign = sign if last else 1.0
    pw, pp = T.ps6, T.ps7
    n = {}

    def inc(ins, name):
        n[name] = n.get(name, 0) + 1
        ins.then_inc(sem[name], 1)
        return name, n[name]

    def wait(q, at):
        q.wait_ge(sem[at[0]], at[1])

    def fr(t, f0, f1, pad=0):
        return t[:, pad + L * f0:pad + L * f1]

    def words(f0, f1):
        return T.bk[:, :].indirect(T.offb[:, K * f0:K * f1])

    def own(f):
        return T.xi[:, 0:PAD + L * f].indirect(T.offp[:, K * f:K * f + K])

    def lower(f):
        return T.lw[:, 0:PAD + L * (f + 1)].indirect(T.offp[:, K * (F + f):K * (F + f) + K])

    lists = 1 if r == 0 else 2

    Y.dma_start(T.pi[LAGS, :], T.par[:, :]).then_inc(sem.par, 16)
    (g if last else A).dma_start(T.pi[GLIDES, :], T.par[:, :]).then_inc(sem.par2, 16)
    Y.dma_start(T.bk[:, :], T.book[:, :]).then_inc(sem.book, 16)

    fl = {"allow_small_or_imprecise_dtypes": True}
    R, UP, DOWN = slice(0, ROWS), slice(0, 32), slice(32, ROWS)
    pat = inc(g.iota(T.pat[R, :], [[-1024, 8], [1, 16]], 31 * 1024, 1024), "iota")
    step = inc(g.iota(T.step[UP, :], [[16, K]], -31 * 1024, 0, **fl), "iota")
    frames = inc(g.iota(T.cf[R, F:(1 + lists) * F], [[0, lists], [L, F]], -MID, 0, **fl), "iota")
    if r:
        ident = inc(g.iota(T.iio[:, :], [[-1, 128]], 0, 1, **fl), "iota")
    else:
        cols = inc(g.iota(T.col[:, :], [[32 * 16, K]], 0, 0, **fl), "iota")
    inc(V.memset(T.step[DOWN, :], 32.0 - 7 * 1024), "vi")
    inc(V.memset(T.cf[UP, 0:F], 32.0), "vi")
    filled = inc(V.memset(T.cf[DOWN, 0:F], -float(MID)), "vi")
    inc(V.memset(T.xi[:, 0:PAD], 0), "vi")
    if r:
        inc(V.memset(T.lw[:, 0:PAD], 0.5), "vi")
    wait(V, pat)
    inc(V.tensor_scalar(T.msk[UP, :], T.pat[UP, :], 31 * 1024 + 15, None, op.bitwise_and), "vi")
    masked = inc(V.tensor_scalar(T.msk[DOWN, :], T.pat[DOWN, :], 7 * 1024, None, op.bitwise_and), "vi")
    wait(V, frames)
    wait(V, filled)
    copied = inc(V.tensor_copy(T.rhs[R, 0:(1 + lists) * F], T.cf[R, 0:(1 + lists) * F]), "vi")
    for q in (V, A):
        wait(q, masked)
        wait(q, step)
    lh_at = {}
    for m in range(K):
        out = T.lh[R, 128 * m:128 * m + 128]
        if m < LH_VECTOR:
            lh_at[m] = inc(V.tensor_scalar(out, T.msk[R, :], T.step[R, m:m + 1], 0.0, op.add, op.max), "lhv")
        else:
            lh_at[m] = inc(A.activation(out, T.msk[R, :], Relu, bias=T.step[R, m:m + 1]), "lhs")
    wait(V, copied)

    V.wait_ge(sem.par, 16)
    conv_w = inc(V.tensor_scalar(T.rhs[LAGS, 0:F], T.pi[LAGS, 0:F], float(L), float(MID), op.mult, op.add), "conv")
    for j in range(lists):
        for rows, table, less in ((LAGS, 1 + 2 * j, MID), (GLIDES, 2 + 2 * j, 32)):
            if rows == GLIDES:
                V.wait_ge(sem.par2, 16)
            conv_p = inc(V.tensor_scalar(T.rhs[rows, (1 + j) * F:(2 + j) * F], T.pi[rows, table * F:(table + 1) * F],
                                         float(less), -1.0, op.subtract, op.mult), "conv")

    def spread(bank, c0, c1):
        for m in range(K):
            if m in lh_at:
                wait(P, lh_at.pop(m))
            ins = P.matmul(bank[:, m:K * (c1 - c0):K], T.lh[R, 128 * m:128 * m + 128], T.rhs[R, c0:c1], True, True)
        return inc(ins, "mm")

    def cast_words(f0, f1):
        return inc(V.tensor_scalar(T.offb[:, K * f0:K * f1], pw[:, K * f0:K * f1], 1 / 32, None, op.mult), "off")

    def cast_places(bank, at, c0, c1):
        return inc(V.tensor_scalar(T.offp[:, c0:c1], bank[:, at + c0:at + c1], 1 / 32, PAD + 31 / 64,
                                   op.mult, op.add), "off")

    def chain(f):
        return inc(V.tensor_tensor(fr(T.xi, f, f + 1, PAD), own(f), fr(T.pre, f, f + 1), op.add), "done")

    x_at, z_at = {}, {}

    def clean(f):
        wait(A, x_at[f])
        z_at[f] = inc(A.activation(fr(T.z, f, f + 1), fr(T.xi, f, f + 1, PAD), Copy, bias=0.5, scale=zsign / SCALE), "zs")

    A.wait_ge(sem.book, 16)
    if r == 0:
        wait(P, conv_w)
        wait(P, lh_at[0])
        wait(V, inc(P.matmul(T.ps0[:, 0:QUICK], T.lh[R, 0:128], T.rhs[R, 0:QUICK], True, True), "mm"))
        wait(P, conv_p)
        spread_p = spread(pw, 0, 2 * F)
        wait(V, cols)
        quick = [inc(V.tensor_scalar(T.offb[:, K * f:K * f + K], T.col[:, :], T.ps0[:, f:f + 1], 1 / 32,
                                     op.add, op.mult), "off") for f in range(QUICK)]
        wait(V, quick[0])
        wait(A, quick[0])
        V.wait_ge(sem.book, 16)
        x_at[0] = inc(V.tensor_scalar(fr(T.xi, 0, 1, PAD), words(0, 1), SCALE, None, op.mult), "done")
        z_at[0] = inc(A.activation(fr(T.z, 0, 1), words(0, 1), Copy, bias=0.5), "zs")
        wait(V, spread_p)
        pre_at, cast_at = {}, {("w", f): quick[f] for f in range(1, QUICK)}
        cast_at["p", 1] = cast_places(pw, K * F, K, K * FIRST)
        cast_at["w", QUICK] = cast_words(QUICK, FIRST)
        more = [FIRST, (FIRST + F) // 2, F]

        def word(f):
            if ("w", f) in cast_at:
                wait(A, cast_at["w", f])
            pre_at[f] = inc(A.activation(fr(T.pre, f, f + 1), words(f, f + 1), Copy, scale=SCALE), "bws")

        for f in range(1, 1 + AHEAD0):
            word(f)
        for f in range(1, F):
            if ("p", f) in cast_at:
                wait(V, cast_at["p", f])
            wait(V, pre_at[f])
            wait(V, x_at[f - 1])
            x_at[f] = chain(f)
            if f <= 2 * (len(more) - 1):
                f0, f1 = more[(f - 1) // 2:(f - 1) // 2 + 2]
                if f % 2:
                    cast_at["w", f0] = cast_words(f0, f1)
                else:
                    cast_at["p", f0] = cast_places(pw, K * F, K * f0, K * f1)
            clean(f)
            if f + AHEAD0 < F:
                word(f + AHEAD0)
    else:
        late_v, late_s = (LATE_VECTOR, LATE_SCALAR) if r == 1 else (0, 0)
        early = F - late_v - late_s

        def words_v(f0, f1):
            return inc(V.tensor_scalar(fr(T.bw, f0, f1), words(f0, f1), sign, None, op.mult), "bwv")

        def words_s(f0, f1):
            return inc(A.activation(fr(T.bw, f0, f1), words(f0, f1), Copy, scale=sign), "bws")

        wait(P, conv_w)
        spread_w = spread(pw, 0, F)
        wait(P, conv_p)
        spread_p = spread(pp, F, 3 * F)
        wait(V, spread_w)
        offb = cast_words(0, F)
        wait(V, spread_p)
        offp = cast_places(pp, 0, 0, 2 * K * F)
        wait(V, ident)
        for j, part in enumerate(SCALES):
            scaled = inc(V.tensor_scalar(T.ident[:, 128 * j:128 * j + 128], T.iio[:, :], 0.0, part,
                                         op.is_equal, op.mult), "vi")
        if last:
            wait(Y, inc(V.memset(T.half[:, :], -0.5), "half"))
            Y.wait_ge(sem.book, 16)
            for f in range(0, ADDED, PIECE):
                Y.dma_start(fr(T.y, f, f + PIECE), T.half[:, :]).then_inc(sem.fill, 16)
        wait(A, offb)
        wait(V, offb)
        V.wait_ge(sem.book, 16)
        word_at = {}
        for b in range(F // BANK):
            word_at[b] = [(words_v if b < BANKS_VECTOR else words_s)(BANK * b, min(BANK * b + BANK, early))]
        wait(V, offp)
        wait(V, word_at[0][0])
        wait(A, offp)

        engines = len(topo.engines(T.cores[r - 1], core))
        V.wait_ge(sem.arr0, engines)
        wait(V, inc(V.tensor_tensor(T.tmp[:, :], lower(0), fr(T.bw, 0, 1), op.add), "low"))
        if not last:
            z_at[0] = inc(V.tensor_scalar(fr(T.z, 0, 1), T.tmp[:, :], -126.5, 127.5, op.max, op.min), "zv")
        x_at[0] = inc(V.tensor_scalar(fr(T.xi, 0, 1, PAD), T.tmp[:, :], 0.5, SCALE, op.subtract, op.mult), "done")
        if late_v:
            word_at[F // BANK - 1].append(words_v(early, early + late_v))

        lg_at, pre_at, bank_at = {}, {}, {}

        def low(f):
            A.wait_ge(sem["arr%d" % f], engines)
            lg_at[f] = inc(A.activation(fr(T.lg, f, f + 1), lower(f), Copy, bias=-0.5 * SCALE, scale=SCALE), "lg")

        def pre(f):
            if f == 1 or f % BANK == 0:
                wait(V, bank_at[f // BANK])
            wait(V, lg_at[f])
            pre_at[f] = inc(V.tensor_tensor(fr(T.pre, f, f + 1), fr(T.lg, f, f + 1),
                                            fr(T["ps%d" % (f // BANK)], f % BANK, f % BANK + 1), op.add), "pre")

        A.wait_ge(sem.arr0, engines)
        for f in range(1, LEAD_LOW + 1):
            low(f)
            if f == 2 and late_s:
                word_at[F // BANK - 1].append(words_s(F - late_s, F))

        wait(P, scaled)
        wait(P, offp)
        for b in range(F // BANK):
            for at in word_at[b]:
                wait(P, at)
            for j in range(len(SCALES)):
                ins = P.matmul(T["ps%d" % b][:, :], T.ident[:, 128 * j:128 * j + 128], fr(T.bw, BANK * b, BANK * b + BANK),
                               j == 0, j == len(SCALES) - 1)
            bank_at[b] = inc(ins, "pe")

        for f in range(1, LEAD_PRE + 1):
            pre(f)
        if last:
            clean(0)
        for f in range(1, F):
            wait(V, x_at[f - 1])
            wait(V, pre_at[f])
            x_at[f] = chain(f)
            if f + LEAD_PRE < F:
                pre(f + LEAD_PRE)
            clean(f)
            if f + LEAD_LOW < F:
                low(f + LEAD_LOW)

    ysign = 1.0 if last else sign

    def whole_v(f0, f1):
        wait(V, z_at[f1 - 1])
        return inc(V.tensor_scalar(fr(T.yf, f0, f1), fr(T.z, f0, f1), 0.5, ysign, op.subtract, op.mult), "yv")

    def whole_s(f0, f1):
        wait(A, z_at[f1 - 1])
        return inc(A.activation(fr(T.yf, f0, f1), fr(T.z, f0, f1), Copy, bias=-0.5 * ysign, scale=ysign), "ys")

    stores = [0]

    def store(q, f0, f1, at):
        wait(q, at)
        q.dma_start(fr(T.y, f0, f1), fr(T.yf, f0, f1)).then_inc(sem.hst, 16)
        stores[0] += 1

    if not last:
        dst = T.cores[r + 1]
        rid, pid, _ = topo.addr(dst)
        mask = topo.mask(core, dst)
        for f in range(F):
            wait(g, z_at[f])
            g.remote_dma(fr(T.lw, f, f + 1, PAD), fr(T.z, f, f + 1), sem["arr%d" % f], sem.sent, pid, rid, mask)
        g.sem_inc(sem.go, 1)
        wait(V, z_at[0])
        wait(A, z_at[0])
        Y.wait_ge(sem.go, 1)
        for j, f in enumerate(range(0, F, PIECE)):
            store(Y, f, f + PIECE, (whole_s if j % 2 else whole_v)(f, f + PIECE))
        g.wait_ge(sem.sent, F * len(topo.engines(core, dst)))
    else:
        g.wait_ge(sem.fill, 16 * (ADDED // PIECE))
        for f in range(0, ADDED, PIECE):
            wait(g, z_at[f + PIECE - 1])
            g.dma_start(fr(T.y, f, f + PIECE), fr(T.z, f, f + PIECE), accum_op=op.add).then_inc(sem.gst, 16)
        for f0, f1 in ((ADDED, F - 2), (F - 2, F - 1), (F - 1, F)):
            store(Y, f0, f1, whole_v(f0, f1))
        g.wait_ge(sem.gst, 16 * (ADDED // PIECE))
    Y.wait_ge(sem.hst, 16 * stores[0])
